import numpy as np, ml_dtypes
CORES = [122,123,126,250,251,254,378,379,382,506,507,510]
N = 12
R, T = 4096, 256
CAPP = 64
def entries(a): return a.T.reshape(-1)
def pack(v, P): return np.ascontiguousarray(np.asarray(v, np.int32).reshape(-1, P).T)
def lists(rng, how):
    Q = rng.permutation(N * R)[:N * T]
    if how == "hotrank": Q = R * int(rng.integers(N)) + rng.permutation(R)[:N * T]
    if how == "own": Q = np.concatenate([R * r + rng.permutation(R)[:T] for r in range(N)])
    if how == "sorted": Q = np.sort(Q)
    if how == "edge":
        ends = np.concatenate([R * np.arange(N), R * np.arange(N) + R - 1]); rest = np.setdiff1d(rng.permutation(N * R), ends, assume_unique=True)
        Q = rng.permutation(np.concatenate([ends, rng.permutation(rest)[:N * T - 2 * N]]))
    if how in ("uniform", "full", "sorted", "edge"):
        O = np.stack([rng.permutation(np.repeat(rng.permutation(N)[:T // CAPP], CAPP)) if how == "full" else rng.permutation(np.repeat(np.arange(N), CAPP))[:T] for r in range(N)]).reshape(-1); Q = np.zeros(N * T, np.int64)
        for d in range(N):
            m = np.nonzero(O == d)[0]; w = rng.permutation(R)[:len(m)]
            if how == "edge" and len(m) >= 2: w[:2] = [0, R - 1]; w[2:] = 1 + rng.permutation(R - 2)[:len(m) - 2]
            Q[m] = R * d + w
        if how == "sorted": Q = np.sort(Q.reshape(N, T), axis=1).reshape(-1)
    return {"pos": np.stack([pack(q, 16) for q in Q.reshape(N, T)])}
def setup_inputs(rng):
    return dict({"tab": rng.standard_normal((N, 128, R), dtype=np.float32).astype(ml_dtypes.bfloat16), "new": rng.standard_normal((N, 128, T), dtype=np.float32).astype(ml_dtypes.bfloat16)}, **lists(rng, "uniform"))
def setup_inputs_edge(rng):
    d = setup_inputs(rng); d.update(lists(rng, "edge"))
    for k in ("tab", "new"): d[k] = (d[k].astype(np.float32) * 1048576.0).astype(d[k].dtype)
    return d
def setup_inputs_full(rng):
    d = setup_inputs(rng); d.update(lists(rng, "full"))
    for k in ("tab", "new"): d[k] = (d[k].astype(np.float32) * (1 / 1024.0)).astype(d[k].dtype)
    return d
def setup_inputs_sorted(rng):
    d = setup_inputs(rng); d.update(lists(rng, "sorted"))
    return d
def check_inputs(x):
    bad = []
    if x["pos"].min() < 0 or x["pos"].max() >= N * R: bad.append("pos out of range")
    if len(np.unique(x["pos"])) != x["pos"].size: bad.append("a place is named twice")
    if max(int(np.bincount(entries(a) // R, minlength=N).max()) for a in x["pos"]) > CAPP: bad.append("more than CAPP entries of a list point into one rank's part")
    return bad
def reference(tab, new, pos):
    A = np.concatenate(list(tab), axis=1)
    for r in range(N): A[:, entries(pos[r])] = new[r]
    return {"y": np.stack([A[:, R * r:R * r + R] for r in range(N)])}

@@ -1,0 +1,270 @@
+from concourse.bass import DstId, RemoteDMATransfer
+from concourse.mybir import AluOpType, AxisListType, ActivationFunctionType
+
+N, RC, CAP = 12, 4096, 64
+W = CAP + 8
+
+SCRATCH = {
+    "tabw": ("sbuf", [128, RC + CAP], "bfloat16"),
+    "newb": ("sbuf", [128, 256], "bfloat16"),
+    "pay": ("sbuf", [128, N * W], "bfloat16"),
+    "land": ("sbuf", [128, N * W], "bfloat16"),
+    "col": ("sbuf", [128, 2], "int32"),
+    "di": ("sbuf", [128, 2], "int32"),
+    "yi": ("sbuf", [128, 4], "int32"),
+    "ui": ("sbuf", [128, 2], "int32"),
+    "abi": ("sbuf", [128, 4], "int32"),
+    "pidx": ("sbuf", [128, 4], "int32"),
+    "tmi": ("sbuf", [128, 8], "int32"),
+    "df": ("sbuf", [128, 2], "float32"),
+    "d64": ("sbuf", [128, 2], "float32"),
+    "af": ("sbuf", [128, 2], "float32"),
+    "lof": ("sbuf", [128, 2], "float32"),
+    "bf": ("sbuf", [128, 2], "float32"),
+    "jf": ("sbuf", [128, 2], "float32"),
+    "rk": ("sbuf", [128, 2], "float32"),
+    "abf": ("sbuf", [128, 4], "float32"),
+    "bc": ("sbuf", [128, 8], "float32"),
+    "r16": ("sbuf", [128, 4], "float32"),
+    "h16": ("sbuf", [128, 2], "float32"),
+    "i12": ("sbuf", [128, 12], "float32"),
+    "i48": ("sbuf", [128, 48], "float32"),
+    "tidx": ("sbuf", [128, 128], "float32"),
+    "ones": ("sbuf", [128, 128], "bfloat16"),
+    "ltb": ("sbuf", [128, 128], "bfloat16"),
+    "oh": ("sbuf", [128, 24], "bfloat16"),
+    "lh": ("sbuf", [128, 256], "bfloat16"),
+    "rh": ("sbuf", [128, 288], "bfloat16"),
+    "gl": ("sbuf", [128, 48], "uint16"),
+    "off": ("sbuf", [128, 48], "uint16"),
+    "ps1": ("psum", [128, 512], "float32"),
+    "psg": ("psum", [128, 512], "float32"),
+    "psab": ("psum", [128, 512], "float32"),
+}
+SEMAPHORES = ["vs", "as_", "ps", "cs", "spos", "snew", "stab", "sout", "sent"] + ["arr%d" % s for s in range(N)]
+
+RELAY_PICK = (0, 4, 2)
+
+
+def _engines(mask):
+    return [e for e in range(16) if (mask >> e) & 1]
+
+
+def _bits(es):
+    m = 0
+    for e in es:
+        m |= 1 << e
+    return m
+
+
+def _cnt(mask):
+    return len(_engines(mask))
+
+
+def _plan(s, cores, topo):
+    c = cores[s]
+    home = [d for d in range(N) if topo.host(cores[d]) == topo.host(c)]
+    peers = [d for d in home if d != s]
+    adj = [d for d in range(N) if d not in home and topo.may_write(c, cores[d])]
+    diag = [d for d in range(N) if not topo.may_write(c, cores[d])]
+    a = home.index(s)
+    near = [d for d in adj if topo.rack(topo.host(cores[d])) == topo.rack(topo.host(c))]
+    far = [d for d in adj if d not in near]
+    via = (far if a == 1 else near)[0]
+    idle = [x for x in range(max(cores) + 8) if topo.host(x) == topo.host(cores[via])
+            and topo.chip(x) == topo.chip(cores[via]) and x not in cores]
+    relay = idle[RELAY_PICK[a]]
+    offm = topo.mask(c, cores[adj[0]])
+    oe = _engines(offm)
+    pe = _engines(topo.mask(c, cores[peers[0]]) & ~offm)
+    eng = {}
+    for k, d in enumerate(adj[0:4]):
+        eng[d] = _bits(oe[2 * k:2 * k + 2])
+    for k, d in enumerate(adj[4:6]):
+        eng[d] = _bits(oe[4 * k:4 * k + 4])
+    for k, d in enumerate(peers):
+        eng[d] = _bits(pe[4 * k:4 * k + 4])
+    for d in diag:
+        eng[d] = topo.mask(relay, cores[d])
+    return {"peers": peers, "adj": adj, "diag": diag, "relay": relay, "eng": eng}
+
+
+def rank_program(g, core, T, topo):
+    cores = list(T.cores)
+    plans = [_plan(s, cores, topo) for s in range(N)]
+    rank = T.rank_of(core)
+    S = T.sem
+    A = AluOpType
+
+    if rank is None:
+        for s in range(N):
+            P = plans[s]
+            if P["relay"] != core:
+                continue
+            g.wait_ge(S["arr%d" % s], _cnt(topo.mask(cores[s], core)))
+            cnt = 0
+            for k, d in enumerate(P["diag"]):
+                rid, pid = topo.addr(cores[d], core)
+                g.remote_dma(T.land[:, W * s:W * s + W], T.land[:, W * k:W * k + W], S["arr%d" % s], S.sent, pid, rid,
+                             P["eng"][d])
+                cnt += _cnt(P["eng"][d])
+            g.wait_ge(S.sent, cnt)
+        return
+
+    P = plans[rank]
+    n = {"v": 0, "a": 0, "c": 0}
+
+    def V(fn, deps=()):
+        for sem, val in deps:
+            g.vector.wait_ge(sem, val)
+        if n["v"]:
+            g.vector.wait_ge(S.vs, n["v"])
+        fn().then_inc(S.vs, 1)
+        n["v"] += 1
+
+    def AC(fn, deps=()):
+        for sem, val in deps:
+            g.scalar.wait_ge(sem, val)
+        if n["a"]:
+            g.scalar.wait_ge(S.as_, n["a"])
+        fn().then_inc(S.as_, 1)
+        n["a"] += 1
+
+    def C(fn, deps=()):
+        for sem, val in deps:
+            g.wait_ge(sem, val)
+        if n["c"]:
+            g.wait_ge(S.cs, n["c"])
+        fn().then_inc(S.cs, 1)
+        n["c"] += 1
+
+    v = g.vector
+    g.scalar.dma_start(T.col[:, :], T.pos[:, :]).then_inc(S.spos, 16)
+    g.sync.dma_start(T.newb[:, :], T.new[:, :]).then_inc(S.snew, 16)
+    g.sync.dma_start(T.tabw[:, 0:RC], T.tab[:, :]).then_inc(S.stab, 16)
+
+    V(lambda: v.memset(T.ones[:, :], 1.0))
+    V(lambda: v.memset(T.bc[:, 0:4], 4096.0))
+    C(lambda: g.iota(T.pidx[:, :], [[0, 4]], 0, 1))
+    C(lambda: g.iota(T.r16[:, :], [[16, 4]], 0, 0, allow_small_or_imprecise_dtypes=True))
+    C(lambda: g.iota(T.h16[:, :], [[16, 2]], 0, 0, allow_small_or_imprecise_dtypes=True))
+    c_small = n["c"]
+    C(lambda: g.iota(T.i12[:, :], [[1, 12]], 0, 0, allow_small_or_imprecise_dtypes=True))
+    C(lambda: g.affine_select(T.ltb[:, :], T.ones[:, :], [[1, 128]], A.is_gt, 0.0, 0, -1), [(S.vs, 1)])
+    C(lambda: g.affine_select(T.ltb[:, :], T.ltb[:, :], [[1, 128]], A.not_equal, 64.0, 0, -1))
+    c_ltb = n["c"]
+    C(lambda: g.iota(T.i48[:, :], [[1, 48]], 4, 0, allow_small_or_imprecise_dtypes=True))
+    C(lambda: g.iota(T.tidx[:, :], [[0, 8], [1, 16]], 0, 0, allow_small_or_imprecise_dtypes=True))
+    c_all = n["c"]
+    V(lambda: v.tensor_scalar(out=T.tmi[:, 0:4], in0=T.pidx[:, :], scalar1=15, scalar2=None, op0=A.bitwise_and),
+      [(S.cs, c_small)])
+    V(lambda: v.tensor_tensor(out=T.bc[:, 4:8], in0=T.tmi[:, 0:4], in1=T.r16[:, :], op=A.add))
+    v_bc = n["v"]
+    V(lambda: v.tensor_scalar(out=T.tmi[:, 4:6], in0=T.pidx[:, 0:2], scalar1=7, scalar2=None, op0=A.bitwise_and))
+    V(lambda: v.tensor_scalar(out=T.tmi[:, 6:8], in0=T.pidx[:, 0:2], scalar1=3, scalar2=None,
+                              op0=A.logical_shift_right))
+    V(lambda: v.tensor_scalar(out=T.jf[:, :], in0=T.tmi[:, 4:6], scalar1=32.0, scalar2=None, op0=A.mult))
+    V(lambda: v.tensor_tensor(out=T.jf[:, :], in0=T.jf[:, :], in1=T.tmi[:, 6:8], op=A.add))
+    V(lambda: v.tensor_tensor(out=T.jf[:, :], in0=T.jf[:, :], in1=T.h16[:, :], op=A.add))
+
+    V(lambda: v.tensor_scalar(out=T.di[:, :], in0=T.col[:, :], scalar1=12, scalar2=None, op0=A.logical_shift_right),
+      [(S.spos, 16)])
+    V(lambda: v.tensor_copy(out=T.df[:, :], in_=T.di[:, :]))
+    V(lambda: v.tensor_scalar(out=T.oh[:, 0:12], in0=T.i12[:, :], scalar1=T.df[:, 0:1], scalar2=None, op0=A.is_equal),
+      [(S.cs, c_ltb)])
+    g.tensor.wait_ge(S.cs, c_ltb)
+    g.tensor.wait_ge(S.vs, n["v"])
+    g.tensor.matmul(T.ps1[:, 0:12], T.ltb[:, :], T.oh[:, 0:12], True, True).then_inc(S.ps, 1)
+    g.tensor.matmul(T.ps1[:, 12:24], T.ones[:, :], T.oh[:, 0:12], True, False)
+    V(lambda: v.tensor_scalar(out=T.oh[:, 12:24], in0=T.i12[:, :], scalar1=T.df[:, 1:2], scalar2=None, op0=A.is_equal))
+    g.tensor.wait_ge(S.vs, n["v"])
+    g.tensor.matmul(T.ps1[:, 12:24], T.ltb[:, :], T.oh[:, 12:24], False, True).then_inc(S.ps, 1)
+    V(lambda: v.tensor_scalar(out=T.yi[:, 0:2], in0=T.col[:, :], scalar1=4032, scalar2=None, op0=A.bitwise_and))
+    V(lambda: v.tensor_scalar(out=T.yi[:, 2:4], in0=T.col[:, :], scalar1=63, scalar2=None, op0=A.bitwise_and))
+    V(lambda: v.tensor_scalar(out=T.d64[:, :], in0=T.df[:, :], scalar1=64.0, scalar2=None, op0=A.mult))
+    V(lambda: v.tensor_scalar(out=T.af[:, :], in0=T.yi[:, 0:2], scalar1=-4032.0, scalar2=None, op0=A.add))
+    V(lambda: v.tensor_copy(out=T.lof[:, :], in_=T.yi[:, 2:4]))
+    V(lambda: v.tensor_reduce(out=T.rk[:, 0:1], in_=T.ps1[:, 0:12], axis=AxisListType.X, op=A.max), [(S.ps, 2)])
+    V(lambda: v.tensor_reduce(out=T.rk[:, 1:2], in_=T.ps1[:, 12:24], axis=AxisListType.X, op=A.max))
+    V(lambda: v.tensor_tensor(out=T.ui[:, :], in0=T.rk[:, :], in1=T.d64[:, :], op=A.add))
+    V(lambda: v.tensor_scalar(out=T.abi[:, 0:2], in0=T.ui[:, :], scalar1=4, scalar2=None, op0=A.logical_shift_right))
+    V(lambda: v.tensor_scalar(out=T.abi[:, 2:4], in0=T.ui[:, :], scalar1=15, scalar2=None, op0=A.bitwise_and))
+    V(lambda: v.tensor_copy(out=T.abf[:, :], in_=T.abi[:, :]))
+    V(lambda: v.tensor_tensor(out=T.bf[:, :], in0=T.lof[:, :], in1=T.rk[:, :], op=A.subtract))
+
+    vals = (T.jf, T.af, T.bf)
+    for h in range(2):
+        V(lambda: v.tensor_scalar(out=T.lh[:, 128 * h:128 * h + 128], in0=T.tidx[:, :], scalar1=T.abf[:, 2 + h:3 + h],
+                                  scalar2=None, op0=A.is_equal), [(S.cs, c_all)])
+        for q in range(3):
+            V(lambda: v.tensor_scalar(out=T.rh[:, 144 * h + 48 * q:144 * h + 48 * q + 48], in0=T.i48[:, :],
+                                      scalar1=T.abf[:, h:h + 1], scalar2=vals[q][:, h:h + 1], op0=A.is_equal,
+                                      op1=A.mult))
+        g.tensor.wait_ge(S.vs, n["v"])
+        m1 = g.tensor.matmul(T.psg[:, 0:48], T.lh[:, 128 * h:128 * h + 128], T.rh[:, 144 * h:144 * h + 48], h == 0, h == 1)
+        m2 = g.tensor.matmul(T.psab[:, 0:96], T.lh[:, 128 * h:128 * h + 128], T.rh[:, 144 * h + 48:144 * h + 144],
+                             h == 0, h == 1)
+        if h == 1:
+            m1.then_inc(S.ps, 1)
+            m2.then_inc(S.ps, 1)
+
+    V(lambda: v.tensor_copy(out=T.gl[:, :], in_=T.psg[:, 0:48]), [(S.ps, 4)])
+    v_gl = n["v"]
+    for k in range(8):
+        AC(lambda: g.scalar.activation(T.pay[:, CAP + k::W], T.psab[:, 48 * (k // 4) + k % 4:48 * (k // 4) + 48:4],
+                                       ActivationFunctionType.Identity, bias=T.bc[:, k:k + 1]),
+           [(S.ps, 4), (S.vs, v_bc)] if k == 0 else ())
+    a_off = n["a"]
+    order = P["diag"] + P["adj"] + P["peers"] + [rank]
+    ready = {}
+    for k, d in enumerate(order):
+        if k < 8:
+            V(lambda: v.tensor_copy(out=T.pay[:, W * d:W * d + CAP], in_=T.newb[:, 0:256].indirect(T.gl[:, 4 * d:4 * d + 4])),
+              [(S.snew, 16)] if k == 0 else ())
+            ready[d] = ("v", n["v"])
+        else:
+            AC(lambda: g.scalar.activation(T.pay[:, W * d:W * d + CAP], T.newb[:, 0:256].indirect(T.gl[:, 4 * d:4 * d + 4]),
+                                           ActivationFunctionType.Copy), [(S.snew, 16), (S.vs, v_gl)] if k == 8 else ())
+            ready[d] = ("a", n["a"])
+
+    def wait_ready(ds):
+        best = {"v": 0, "a": a_off}
+        for d in ds:
+            tag, val = ready[d]
+            best[tag] = max(best[tag], val)
+        if best["v"]:
+            g.wait_ge(S.vs, best["v"])
+        g.wait_ge(S.as_, best["a"])
+
+    sent = 0
+    me = "arr%d" % rank
+    d0 = min(P["diag"])
+    wait_ready(P["diag"])
+    rid, pid = topo.addr(P["relay"], core)
+    rm = topo.mask(core, P["relay"])
+    g.remote_dma(T.land[:, 0:3 * W], T.pay[:, W * d0:W * d0 + 3 * W], S[me], S.sent, pid, rid, rm)
+    sent += _cnt(rm)
+    for ds in (P["adj"][0:4], P["adj"][4:6], P["peers"]):
+        wait_ready(ds)
+        trs = []
+        for d in ds:
+            rid, pid = topo.addr(cores[d], core)
+            trs.append(RemoteDMATransfer(dst_ids=[DstId(rid=rid, pnc=pid)], dma_engine_mask=P["eng"][d], remote_sem=S[me],
+                                         src=T.pay[:, W * d:W * d + W], dst=T.land[:, W * rank:W * rank + W]))
+            sent += _cnt(P["eng"][d])
+        g.remote_dma_fused(trs, local_sem=S.sent)
+
+    first = True
+    for s in [rank] + P["peers"] + P["adj"] + P["diag"]:
+        buf = T.pay if s == rank else T.land
+        deps = [(S.as_, n["a"])] if s == rank else [(S["arr%d" % s], _cnt(plans[s]["eng"][rank]))]
+        V(lambda: v.tensor_tensor(out=T.off[:, 4 * s:4 * s + 4], in0=buf[:, W * s + CAP:W * s + CAP + 4],
+                                  in1=buf[:, W * s + CAP + 4:W * s + CAP + 8], op=A.add), deps)
+        V(lambda: v.tensor_copy(out=T.tabw[:, 0:RC + CAP].indirect(T.off[:, 4 * s:4 * s + 4]),
+                                in_=buf[:, W * s:W * s + CAP]), [(S.stab, 16)] if first else ())
+        first = False
+
+    g.sync.wait_ge(S.vs, n["v"])
+    g.sync.dma_start(T.y[:, :], T.tabw[:, 0:RC]).then_inc(S.sout, 16)
+    g.sync.wait_ge(S.sout, 16)
+    g.wait_ge(S.sent, sent)

@@ -12,21 +12,20 @@ SCRATCH = {
     "col": ("sbuf", [128, 2], "int32"),
     "di": ("sbuf", [128, 2], "int32"),
     "yi": ("sbuf", [128, 4], "int32"),
-    "ui": ("sbuf", [128, 2], "int32"),
-    "abi": ("sbuf", [128, 4], "int32"),
+    "r16i": ("sbuf", [128, 2], "int32"),
     "pidx": ("sbuf", [128, 4], "int32"),
     "tmi": ("sbuf", [128, 8], "int32"),
     "df": ("sbuf", [128, 2], "float32"),
-    "d64": ("sbuf", [128, 2], "float32"),
+    "d4": ("sbuf", [128, 2], "float32"),
     "af": ("sbuf", [128, 2], "float32"),
     "lof": ("sbuf", [128, 2], "float32"),
     "bf": ("sbuf", [128, 2], "float32"),
     "jf": ("sbuf", [128, 2], "float32"),
+    "jb": ("sbuf", [128, 2], "float32"),
     "rk": ("sbuf", [128, 2], "float32"),
     "abf": ("sbuf", [128, 4], "float32"),
     "bc": ("sbuf", [128, 8], "float32"),
     "r16": ("sbuf", [128, 4], "float32"),
-    "h16": ("sbuf", [128, 2], "float32"),
     "i12": ("sbuf", [128, 12], "float32"),
     "i48": ("sbuf", [128, 48], "float32"),
     "tidx": ("sbuf", [128, 128], "float32"),
@@ -41,7 +40,8 @@ SCRATCH = {
     "psg": ("psum", [128, 512], "float32"),
     "psab": ("psum", [128, 512], "float32"),
 }
-SEMAPHORES = ["vs", "as_", "ps", "cs", "spos", "snew", "stab", "sout", "sent"] + ["arr%d" % s for s in range(N)]
+SEMAPHORES = ["vs", "on", "c1", "c2", "c3", "p1", "h0", "h1", "p2", "gls", "ab", "gd", "g4", "g2", "gp", "go",
+              "spos", "snew", "stab", "sout", "sent"] + ["arr%d" % s for s in range(N)]
 
 RELAY_PICK = (0, 4, 2)
 
@@ -112,157 +112,147 @@ def rank_program(g, core, T, topo):
         return
 
     P = plans[rank]
-    n = {"v": 0, "a": 0, "c": 0}
+    v, pe, ac = g.vector, g.tensor, g.scalar
+    n = {"v": 0}
 
-    def V(fn, deps=()):
+    def level(*deps):
         for sem, val in deps:
-            g.vector.wait_ge(sem, val)
+            v.wait_ge(sem, val)
         if n["v"]:
-            g.vector.wait_ge(S.vs, n["v"])
-        fn().then_inc(S.vs, 1)
+            v.wait_ge(S.vs, n["v"])
+
+    def V(inst):
+        inst.then_inc(S.vs, 1)
         n["v"] += 1
 
-    def AC(fn, deps=()):
-        for sem, val in deps:
-            g.scalar.wait_ge(sem, val)
-        if n["a"]:
-            g.scalar.wait_ge(S.as_, n["a"])
-        fn().then_inc(S.as_, 1)
-        n["a"] += 1
+    def ts(out, in0, s1, op0, s2=None, op1=None):
+        if op1 is None:
+            return v.tensor_scalar(out=out, in0=in0, scalar1=s1, scalar2=None, op0=op0)
+        return v.tensor_scalar(out=out, in0=in0, scalar1=s1, scalar2=s2, op0=op0, op1=op1)
 
-    def C(fn, deps=()):
-        for sem, val in deps:
-            g.wait_ge(sem, val)
-        if n["c"]:
-            g.wait_ge(S.cs, n["c"])
-        fn().then_inc(S.cs, 1)
-        n["c"] += 1
-
-    v = g.vector
-    g.scalar.dma_start(T.col[:, :], T.pos[:, :]).then_inc(S.spos, 16)
+    ac.dma_start(T.col[:, :], T.pos[:, :]).then_inc(S.spos, 16)
     g.sync.dma_start(T.newb[:, :], T.new[:, :]).then_inc(S.snew, 16)
     g.sync.dma_start(T.tabw[:, 0:RC], T.tab[:, :]).then_inc(S.stab, 16)
 
-    V(lambda: v.memset(T.ones[:, :], 1.0))
-    V(lambda: v.memset(T.bc[:, 0:4], 4096.0))
-    C(lambda: g.iota(T.pidx[:, :], [[0, 4]], 0, 1))
-    C(lambda: g.iota(T.r16[:, :], [[16, 4]], 0, 0, allow_small_or_imprecise_dtypes=True))
-    C(lambda: g.iota(T.h16[:, :], [[16, 2]], 0, 0, allow_small_or_imprecise_dtypes=True))
-    c_small = n["c"]
-    C(lambda: g.iota(T.i12[:, :], [[1, 12]], 0, 0, allow_small_or_imprecise_dtypes=True))
-    C(lambda: g.affine_select(T.ltb[:, :], T.ones[:, :], [[1, 128]], A.is_gt, 0.0, 0, -1), [(S.vs, 1)])
-    C(lambda: g.affine_select(T.ltb[:, :], T.ltb[:, :], [[1, 128]], A.not_equal, 64.0, 0, -1))
-    c_ltb = n["c"]
-    C(lambda: g.iota(T.i48[:, :], [[1, 48]], 4, 0, allow_small_or_imprecise_dtypes=True))
-    C(lambda: g.iota(T.tidx[:, :], [[0, 8], [1, 16]], 0, 0, allow_small_or_imprecise_dtypes=True))
-    c_all = n["c"]
-    V(lambda: v.tensor_scalar(out=T.tmi[:, 0:4], in0=T.pidx[:, :], scalar1=15, scalar2=None, op0=A.bitwise_and),
-      [(S.cs, c_small)])
-    V(lambda: v.tensor_tensor(out=T.bc[:, 4:8], in0=T.tmi[:, 0:4], in1=T.r16[:, :], op=A.add))
+    v.memset(T.ones[:, :], 1.0).then_inc(S.on, 1)
+    V(v.memset(T.bc[:, 0:4], 4096.0))
+    g.iota(T.pidx[:, :], [[0, 4]], 0, 1).then_inc(S.c1, 1)
+    g.iota(T.jb[:, :], [[16, 2]], 0, 32, allow_small_or_imprecise_dtypes=True).then_inc(S.c1, 1)
+    g.iota(T.r16[:, :], [[16, 4]], 0, 0, allow_small_or_imprecise_dtypes=True).then_inc(S.c1, 1)
+    g.iota(T.i12[:, :], [[1, 12]], 0, 0, allow_small_or_imprecise_dtypes=True).then_inc(S.c2, 1)
+    g.wait_ge(S.on, 1)
+    g.affine_select(T.ltb[:, :], T.ones[:, :], [[1, 128]], A.is_gt, 0.0, 0, -1).then_inc(S.c2, 1)
+    g.wait_ge(S.c2, 2)
+    g.affine_select(T.ltb[:, :], T.ltb[:, :], [[1, 128]], A.not_equal, 64.0, 0, -1).then_inc(S.c2, 1)
+    g.iota(T.i48[:, :], [[1, 48]], 0, 0, allow_small_or_imprecise_dtypes=True).then_inc(S.c3, 1)
+    g.iota(T.tidx[:, :], [[0, 8], [1, 16]], 64, 0, allow_small_or_imprecise_dtypes=True).then_inc(S.c3, 1)
+    level((S.c1, 3))
+    V(ts(T.tmi[:, 0:4], T.pidx[:, :], 15, A.bitwise_and))
+    V(ts(T.tmi[:, 4:6], T.pidx[:, 0:2], 3, A.logical_shift_right))
+    level()
+    V(v.tensor_tensor(out=T.bc[:, 4:8], in0=T.tmi[:, 0:4], in1=T.r16[:, :], op=A.add))
+    V(ts(T.jf[:, :], T.tmi[:, 4:6], -255.0, A.mult))
+    level()
     v_bc = n["v"]
-    V(lambda: v.tensor_scalar(out=T.tmi[:, 4:6], in0=T.pidx[:, 0:2], scalar1=7, scalar2=None, op0=A.bitwise_and))
-    V(lambda: v.tensor_scalar(out=T.tmi[:, 6:8], in0=T.pidx[:, 0:2], scalar1=3, scalar2=None,
-                              op0=A.logical_shift_right))
-    V(lambda: v.tensor_scalar(out=T.jf[:, :], in0=T.tmi[:, 4:6], scalar1=32.0, scalar2=None, op0=A.mult))
-    V(lambda: v.tensor_tensor(out=T.jf[:, :], in0=T.jf[:, :], in1=T.tmi[:, 6:8], op=A.add))
-    V(lambda: v.tensor_tensor(out=T.jf[:, :], in0=T.jf[:, :], in1=T.h16[:, :], op=A.add))
+    V(v.tensor_tensor(out=T.jf[:, :], in0=T.jf[:, :], in1=T.jb[:, :], op=A.add))
 
-    V(lambda: v.tensor_scalar(out=T.di[:, :], in0=T.col[:, :], scalar1=12, scalar2=None, op0=A.logical_shift_right),
-      [(S.spos, 16)])
-    V(lambda: v.tensor_copy(out=T.df[:, :], in_=T.di[:, :]))
-    V(lambda: v.tensor_scalar(out=T.oh[:, 0:12], in0=T.i12[:, :], scalar1=T.df[:, 0:1], scalar2=None, op0=A.is_equal),
-      [(S.cs, c_ltb)])
-    g.tensor.wait_ge(S.cs, c_ltb)
-    g.tensor.wait_ge(S.vs, n["v"])
-    g.tensor.matmul(T.ps1[:, 0:12], T.ltb[:, :], T.oh[:, 0:12], True, True).then_inc(S.ps, 1)
-    g.tensor.matmul(T.ps1[:, 12:24], T.ones[:, :], T.oh[:, 0:12], True, False)
-    V(lambda: v.tensor_scalar(out=T.oh[:, 12:24], in0=T.i12[:, :], scalar1=T.df[:, 1:2], scalar2=None, op0=A.is_equal))
-    g.tensor.wait_ge(S.vs, n["v"])
-    g.tensor.matmul(T.ps1[:, 12:24], T.ltb[:, :], T.oh[:, 12:24], False, True).then_inc(S.ps, 1)
-    V(lambda: v.tensor_scalar(out=T.yi[:, 0:2], in0=T.col[:, :], scalar1=4032, scalar2=None, op0=A.bitwise_and))
-    V(lambda: v.tensor_scalar(out=T.yi[:, 2:4], in0=T.col[:, :], scalar1=63, scalar2=None, op0=A.bitwise_and))
-    V(lambda: v.tensor_scalar(out=T.d64[:, :], in0=T.df[:, :], scalar1=64.0, scalar2=None, op0=A.mult))
-    V(lambda: v.tensor_scalar(out=T.af[:, :], in0=T.yi[:, 0:2], scalar1=-4032.0, scalar2=None, op0=A.add))
-    V(lambda: v.tensor_copy(out=T.lof[:, :], in_=T.yi[:, 2:4]))
-    V(lambda: v.tensor_reduce(out=T.rk[:, 0:1], in_=T.ps1[:, 0:12], axis=AxisListType.X, op=A.max), [(S.ps, 2)])
-    V(lambda: v.tensor_reduce(out=T.rk[:, 1:2], in_=T.ps1[:, 12:24], axis=AxisListType.X, op=A.max))
-    V(lambda: v.tensor_tensor(out=T.ui[:, :], in0=T.rk[:, :], in1=T.d64[:, :], op=A.add))
-    V(lambda: v.tensor_scalar(out=T.abi[:, 0:2], in0=T.ui[:, :], scalar1=4, scalar2=None, op0=A.logical_shift_right))
-    V(lambda: v.tensor_scalar(out=T.abi[:, 2:4], in0=T.ui[:, :], scalar1=15, scalar2=None, op0=A.bitwise_and))
-    V(lambda: v.tensor_copy(out=T.abf[:, :], in_=T.abi[:, :]))
-    V(lambda: v.tensor_tensor(out=T.bf[:, :], in0=T.lof[:, :], in1=T.rk[:, :], op=A.subtract))
+    v.wait_ge(S.spos, 16)
+    V(ts(T.di[:, :], T.col[:, :], 12, A.logical_shift_right))
+    V(ts(T.yi[:, 0:2], T.col[:, :], 4032, A.bitwise_and))
+    V(ts(T.yi[:, 2:4], T.col[:, :], 63, A.bitwise_and))
+    level()
+    V(v.tensor_copy(out=T.df[:, :], in_=T.di[:, :]))
+    V(ts(T.af[:, :], T.yi[:, 0:2], -4032.0, A.add))
+    V(v.tensor_copy(out=T.lof[:, :], in_=T.yi[:, 2:4]))
+    level((S.c2, 3))
+    V(ts(T.oh[:, 0:12], T.i12[:, :], T.df[:, 0:1], A.is_equal))
+    V(ts(T.oh[:, 12:24], T.i12[:, :], T.df[:, 1:2], A.is_equal))
+    V(ts(T.d4[:, :], T.df[:, :], 4.0, A.mult))
+    pe.wait_ge(S.c2, 3)
+    pe.wait_ge(S.on, 1)
+    pe.wait_ge(S.vs, n["v"])
+    pe.matmul(T.ps1[:, 0:12], T.ltb[:, :], T.oh[:, 0:12], True, True).then_inc(S.p1, 1)
+    pe.matmul(T.ps1[:, 12:24], T.ones[:, :], T.oh[:, 0:12], True, False)
+    pe.matmul(T.ps1[:, 12:24], T.ltb[:, :], T.oh[:, 12:24], False, True).then_inc(S.p1, 1)
+    v.wait_ge(S.p1, 2)
+    V(v.tensor_reduce(out=T.rk[:, 0:1], in_=T.ps1[:, 0:12], axis=AxisListType.X, op=A.max))
+    V(v.tensor_reduce(out=T.rk[:, 1:2], in_=T.ps1[:, 12:24], axis=AxisListType.X, op=A.max))
+    level()
+    V(ts(T.r16i[:, :], T.rk[:, :], 0.0625, A.mult, -4.46875, A.add))
+    V(v.tensor_tensor(out=T.bf[:, :], in0=T.lof[:, :], in1=T.rk[:, :], op=A.subtract))
+    level()
+    V(v.tensor_tensor(out=T.abf[:, 0:2], in0=T.r16i[:, :], in1=T.d4[:, :], op=A.add))
+    for h in range(2):
+        V(ts(T.abf[:, 2 + h:3 + h], T.r16i[:, h:h + 1], -16.0, A.mult, T.rk[:, h:h + 1], A.add))
 
+    level((S.c3, 2))
     vals = (T.jf, T.af, T.bf)
     for h in range(2):
-        V(lambda: v.tensor_scalar(out=T.lh[:, 128 * h:128 * h + 128], in0=T.tidx[:, :], scalar1=T.abf[:, 2 + h:3 + h],
-                                  scalar2=None, op0=A.is_equal), [(S.cs, c_all)])
+        hs = S["h%d" % h]
+        ts(T.lh[:, 128 * h:128 * h + 128], T.tidx[:, :], T.abf[:, 2 + h:3 + h], A.is_equal).then_inc(hs, 1)
         for q in range(3):
-            V(lambda: v.tensor_scalar(out=T.rh[:, 144 * h + 48 * q:144 * h + 48 * q + 48], in0=T.i48[:, :],
-                                      scalar1=T.abf[:, h:h + 1], scalar2=vals[q][:, h:h + 1], op0=A.is_equal,
-                                      op1=A.mult))
-        g.tensor.wait_ge(S.vs, n["v"])
-        m1 = g.tensor.matmul(T.psg[:, 0:48], T.lh[:, 128 * h:128 * h + 128], T.rh[:, 144 * h:144 * h + 48], h == 0, h == 1)
-        m2 = g.tensor.matmul(T.psab[:, 0:96], T.lh[:, 128 * h:128 * h + 128], T.rh[:, 144 * h + 48:144 * h + 144],
-                             h == 0, h == 1)
+            ts(T.rh[:, 144 * h + 48 * q:144 * h + 48 * q + 48], T.i48[:, :], T.abf[:, h:h + 1], A.is_equal,
+               vals[q][:, h:h + 1], A.mult).then_inc(hs, 1)
+        pe.wait_ge(hs, 4)
+        m1 = pe.matmul(T.psg[:, 0:48], T.lh[:, 128 * h:128 * h + 128], T.rh[:, 144 * h:144 * h + 48], h == 0, h == 1)
+        m2 = pe.matmul(T.psab[:, 0:96], T.lh[:, 128 * h:128 * h + 128], T.rh[:, 144 * h + 48:144 * h + 144],
+                       h == 0, h == 1)
         if h == 1:
-            m1.then_inc(S.ps, 1)
-            m2.then_inc(S.ps, 1)
+            m1.then_inc(S.p2, 1)
+            m2.then_inc(S.p2, 1)
 
-    V(lambda: v.tensor_copy(out=T.gl[:, :], in_=T.psg[:, 0:48]), [(S.ps, 4)])
-    v_gl = n["v"]
+    v.wait_ge(S.p2, 2)
+    v.tensor_copy(out=T.gl[:, :], in_=T.psg[:, 0:48]).then_inc(S.gls, 1)
+    ac.wait_ge(S.p2, 2)
+    ac.wait_ge(S.vs, v_bc)
     for k in range(8):
-        AC(lambda: g.scalar.activation(T.pay[:, CAP + k::W], T.psab[:, 48 * (k // 4) + k % 4:48 * (k // 4) + 48:4],
-                                       ActivationFunctionType.Identity, bias=T.bc[:, k:k + 1]),
-           [(S.ps, 4), (S.vs, v_bc)] if k == 0 else ())
-    a_off = n["a"]
-    order = P["diag"] + P["adj"] + P["peers"] + [rank]
-    ready = {}
-    for k, d in enumerate(order):
-        if k < 8:
-            V(lambda: v.tensor_copy(out=T.pay[:, W * d:W * d + CAP], in_=T.newb[:, 0:256].indirect(T.gl[:, 4 * d:4 * d + 4])),
-              [(S.snew, 16)] if k == 0 else ())
-            ready[d] = ("v", n["v"])
-        else:
-            AC(lambda: g.scalar.activation(T.pay[:, W * d:W * d + CAP], T.newb[:, 0:256].indirect(T.gl[:, 4 * d:4 * d + 4]),
-                                           ActivationFunctionType.Copy), [(S.snew, 16), (S.vs, v_gl)] if k == 8 else ())
-            ready[d] = ("a", n["a"])
-
-    def wait_ready(ds):
-        best = {"v": 0, "a": a_off}
+        ac.activation(T.pay[:, CAP + k::W], T.psab[:, 48 * (k // 4) + k % 4:48 * (k // 4) + 48:4],
+                      ActivationFunctionType.Identity, bias=T.bc[:, k:k + 1]).then_inc(S.ab, 1)
+    groups = [(P["diag"], S.gd), (P["adj"][0:4], S.g4), (P["adj"][4:6], S.g2), (P["peers"], S.gp), ([rank], S.go)]
+    v.wait_ge(S.gls, 1)
+    v.wait_ge(S.snew, 16)
+    ac.wait_ge(S.gls, 1)
+    ac.wait_ge(S.snew, 16)
+    k = 0
+    for ds, sem in groups:
         for d in ds:
-            tag, val = ready[d]
-            best[tag] = max(best[tag], val)
-        if best["v"]:
-            g.wait_ge(S.vs, best["v"])
-        g.wait_ge(S.as_, best["a"])
+            src = T.newb[:, 0:256].indirect(T.gl[:, 4 * d:4 * d + 4])
+            if k < 8:
+                v.tensor_copy(out=T.pay[:, W * d:W * d + CAP], in_=src).then_inc(sem, 1)
+            else:
+                ac.activation(T.pay[:, W * d:W * d + CAP], src, ActivationFunctionType.Copy).then_inc(sem, 1)
+            k += 1
 
     sent = 0
-    me = "arr%d" % rank
+    me = S["arr%d" % rank]
     d0 = min(P["diag"])
-    wait_ready(P["diag"])
+    g.wait_ge(S.ab, 8)
+    g.wait_ge(S.gd, 3)
     rid, pid = topo.addr(P["relay"], core)
     rm = topo.mask(core, P["relay"])
-    g.remote_dma(T.land[:, 0:3 * W], T.pay[:, W * d0:W * d0 + 3 * W], S[me], S.sent, pid, rid, rm)
+    g.remote_dma(T.land[:, 0:3 * W], T.pay[:, W * d0:W * d0 + 3 * W], me, S.sent, pid, rid, rm)
     sent += _cnt(rm)
-    for ds in (P["adj"][0:4], P["adj"][4:6], P["peers"]):
-        wait_ready(ds)
+    for ds, sem in groups[1:4]:
+        g.wait_ge(sem, len(ds))
         trs = []
         for d in ds:
             rid, pid = topo.addr(cores[d], core)
-            trs.append(RemoteDMATransfer(dst_ids=[DstId(rid=rid, pnc=pid)], dma_engine_mask=P["eng"][d], remote_sem=S[me],
+            trs.append(RemoteDMATransfer(dst_ids=[DstId(rid=rid, pnc=pid)], dma_engine_mask=P["eng"][d], remote_sem=me,
                                          src=T.pay[:, W * d:W * d + W], dst=T.land[:, W * rank:W * rank + W]))
             sent += _cnt(P["eng"][d])
         g.remote_dma_fused(trs, local_sem=S.sent)
 
-    first = True
+    v.wait_ge(S.stab, 16)
     for s in [rank] + P["peers"] + P["adj"] + P["diag"]:
         buf = T.pay if s == rank else T.land
-        deps = [(S.as_, n["a"])] if s == rank else [(S["arr%d" % s], _cnt(plans[s]["eng"][rank]))]
-        V(lambda: v.tensor_tensor(out=T.off[:, 4 * s:4 * s + 4], in0=buf[:, W * s + CAP:W * s + CAP + 4],
-                                  in1=buf[:, W * s + CAP + 4:W * s + CAP + 8], op=A.add), deps)
-        V(lambda: v.tensor_copy(out=T.tabw[:, 0:RC + CAP].indirect(T.off[:, 4 * s:4 * s + 4]),
-                                in_=buf[:, W * s:W * s + CAP]), [(S.stab, 16)] if first else ())
-        first = False
+        if s == rank:
+            level((S.go, 1), (S.ab, 8))
+        else:
+            level((S["arr%d" % s], _cnt(plans[s]["eng"][rank])))
+        V(v.tensor_tensor(out=T.off[:, 4 * s:4 * s + 4], in0=buf[:, W * s + CAP:W * s + CAP + 4],
+                          in1=buf[:, W * s + CAP + 4:W * s + CAP + 8], op=A.add))
+        level()
+        V(v.tensor_copy(out=T.tabw[:, 0:RC + CAP].indirect(T.off[:, 4 * s:4 * s + 4]), in_=buf[:, W * s:W * s + CAP]))
 
     g.sync.wait_ge(S.vs, n["v"])
     g.sync.dma_start(T.y[:, :], T.tabw[:, 0:RC]).then_inc(S.sout, 16)

@@ -28,7 +28,7 @@ SCRATCH = {
     "r16": ("sbuf", [128, 4], "float32"),
     "i12": ("sbuf", [128, 12], "float32"),
     "i48": ("sbuf", [128, 48], "float32"),
-    "tidx": ("sbuf", [128, 128], "float32"),
+    "tidx": ("sbuf", [128, 128], "bfloat16"),
     "ones": ("sbuf", [128, 128], "bfloat16"),
     "ltb": ("sbuf", [128, 128], "bfloat16"),
     "oh": ("sbuf", [128, 24], "bfloat16"),
@@ -246,9 +246,10 @@ def rank_program(g, core, T, topo):
     for s in [rank] + P["peers"] + P["adj"] + P["diag"]:
         buf = T.pay if s == rank else T.land
         if s == rank:
-            level((S.go, 1), (S.ab, 8))
+            v.wait_ge(S.go, 1)
+            v.wait_ge(S.ab, 8)
         else:
-            level((S["arr%d" % s], _cnt(plans[s]["eng"][rank])))
+            v.wait_ge(S["arr%d" % s], _cnt(plans[s]["eng"][rank]))
         V(v.tensor_tensor(out=T.off[:, 4 * s:4 * s + 4], in0=buf[:, W * s + CAP:W * s + CAP + 4],
                           in1=buf[:, W * s + CAP + 4:W * s + CAP + 8], op=A.add))
         level()

@@ -9,6 +9,7 @@ SCRATCH = {
     "newb": ("sbuf", [128, 256], "bfloat16"),
     "pay": ("sbuf", [128, N * W], "bfloat16"),
     "land": ("sbuf", [128, N * W], "bfloat16"),
+    "msg": ("sbuf", [128, 36], "bfloat16"),
     "col": ("sbuf", [128, 2], "int32"),
     "di": ("sbuf", [128, 2], "int32"),
     "yi": ("sbuf", [128, 4], "int32"),
@@ -41,7 +42,7 @@ SCRATCH = {
     "psab": ("psum", [128, 512], "float32"),
 }
 SEMAPHORES = ["vs", "on", "c1", "c2", "c3", "p1", "h0", "h1", "p2", "gls", "ab", "gd", "g4", "g2", "gp", "go",
-              "spos", "snew", "stab", "sout", "sent"] + ["arr%d" % s for s in range(N)]
+              "spos", "snew", "stab", "sout", "sent", "raw", "ms"] + ["arr%d" % s for s in range(N)]
 
 RELAY_PICK = (0, 4, 2)
 
@@ -101,12 +102,40 @@ def rank_program(g, core, T, topo):
             P = plans[s]
             if P["relay"] != core:
                 continue
-            g.wait_ge(S["arr%d" % s], _cnt(topo.mask(cores[s], core)))
+            v, ac = g.vector, g.scalar
+            cm = _cnt(topo.mask(cores[s], core))
+            arr = S["arr%d" % s]
+            v.memset(T.bc[:, 0:4], 4096.0).then_inc(S.vs, 1)
+            g.iota(T.pidx[:, :], [[0, 4]], 0, 1).then_inc(S.c1, 1)
+            g.iota(T.r16[:, :], [[16, 4]], 0, 0, allow_small_or_imprecise_dtypes=True).then_inc(S.c1, 1)
+            v.wait_ge(S.c1, 2)
+            v.tensor_scalar(out=T.tmi[:, 0:4], in0=T.pidx[:, :], scalar1=15, scalar2=None,
+                            op0=A.bitwise_and).then_inc(S.vs, 1)
+            v.wait_ge(S.vs, 2)
+            v.tensor_tensor(out=T.bc[:, 4:8], in0=T.tmi[:, 0:4], in1=T.r16[:, :], op=A.add).then_inc(S.vs, 1)
+            v.wait_ge(S.vs, 3)
+            ac.wait_ge(S.vs, 3)
+            v.wait_ge(arr, cm)
+            v.tensor_copy(out=T.gl[:, 0:12], in_=T.land[:, 0:12]).then_inc(S.gls, 1)
+            for k in range(3):
+                v.tensor_tensor(out=T.pay[:, W * k + CAP + 4:W * k + CAP + 8], in0=T.land[:, 24 + 4 * k:28 + 4 * k],
+                                in1=T.bc[:, 4:8], op=A.add).then_inc(S.ab, 1)
+            ac.wait_ge(arr, cm)
+            for k in range(3):
+                ac.activation(T.pay[:, W * k + CAP:W * k + CAP + 4], T.land[:, 12 + 4 * k:16 + 4 * k],
+                              ActivationFunctionType.Identity, bias=T.bc[:, 0:1]).then_inc(S.ab, 1)
+            v.wait_ge(S.gls, 1)
+            v.wait_ge(S.raw, cm)
+            done = (S.gd, S.g4, S.g2)
+            for k in range(3):
+                v.tensor_copy(out=T.pay[:, W * k:W * k + CAP],
+                              in_=T.newb[:, 0:256].indirect(T.gl[:, 4 * k:4 * k + 4])).then_inc(done[k], 1)
+            g.wait_ge(S.ab, 6)
             cnt = 0
             for k, d in enumerate(P["diag"]):
+                g.wait_ge(done[k], 1)
                 rid, pid = topo.addr(cores[d], core)
-                g.remote_dma(T.land[:, W * s:W * s + W], T.land[:, W * k:W * k + W], S["arr%d" % s], S.sent, pid, rid,
-                             P["eng"][d])
+                g.remote_dma(T.land[:, W * s:W * s + W], T.pay[:, W * k:W * k + W], arr, S.sent, pid, rid, P["eng"][d])
                 cnt += _cnt(P["eng"][d])
             g.wait_ge(S.sent, cnt)
         return
@@ -146,6 +175,16 @@ def rank_program(g, core, T, topo):
     g.affine_select(T.ltb[:, :], T.ltb[:, :], [[1, 128]], A.not_equal, 64.0, 0, -1).then_inc(S.c2, 1)
     g.iota(T.i48[:, :], [[1, 48]], 0, 0, allow_small_or_imprecise_dtypes=True).then_inc(S.c3, 1)
     g.iota(T.tidx[:, :], [[0, 8], [1, 16]], 64, 0, allow_small_or_imprecise_dtypes=True).then_inc(S.c3, 1)
+
+    sent = 0
+    me = S["arr%d" % rank]
+    d0 = min(P["diag"])
+    r_rid, r_pid = topo.addr(P["relay"], core)
+    rm = topo.mask(core, P["relay"])
+    g.wait_ge(S.snew, 16)
+    g.remote_dma(T.newb[:, :], T.newb[:, :], S.raw, S.sent, r_pid, r_rid, rm)
+    sent += _cnt(rm)
+
     level((S.c1, 3))
     V(ts(T.tmi[:, 0:4], T.pidx[:, :], 15, A.bitwise_and))
     V(ts(T.tmi[:, 4:6], T.pidx[:, 0:2], 3, A.logical_shift_right))
@@ -202,13 +241,17 @@ def rank_program(g, core, T, topo):
             m2.then_inc(S.p2, 1)
 
     v.wait_ge(S.p2, 2)
+    v.tensor_copy(out=T.msg[:, 0:12], in_=T.psg[:, 4 * d0:4 * d0 + 12]).then_inc(S.ms, 1)
     v.tensor_copy(out=T.gl[:, :], in_=T.psg[:, 0:48]).then_inc(S.gls, 1)
     ac.wait_ge(S.p2, 2)
+    for q in range(2):
+        ac.activation(T.msg[:, 12 + 12 * q:24 + 12 * q], T.psab[:, 48 * q + 4 * d0:48 * q + 4 * d0 + 12],
+                      ActivationFunctionType.Copy).then_inc(S.ms, 1)
     ac.wait_ge(S.vs, v_bc)
     for k in range(8):
         ac.activation(T.pay[:, CAP + k::W], T.psab[:, 48 * (k // 4) + k % 4:48 * (k // 4) + 48:4],
                       ActivationFunctionType.Identity, bias=T.bc[:, k:k + 1]).then_inc(S.ab, 1)
-    groups = [(P["diag"], S.gd), (P["adj"][0:4], S.g4), (P["adj"][4:6], S.g2), (P["peers"], S.gp), ([rank], S.go)]
+    groups = [(P["adj"][0:4], S.g4), (P["adj"][4:6], S.g2), (P["peers"], S.gp), ([rank], S.go)]
     v.wait_ge(S.gls, 1)
     v.wait_ge(S.snew, 16)
     ac.wait_ge(S.gls, 1)
@@ -217,22 +260,17 @@ def rank_program(g, core, T, topo):
     for ds, sem in groups:
         for d in ds:
             src = T.newb[:, 0:256].indirect(T.gl[:, 4 * d:4 * d + 4])
-            if k < 8:
+            if k < 6:
                 v.tensor_copy(out=T.pay[:, W * d:W * d + CAP], in_=src).then_inc(sem, 1)
             else:
                 ac.activation(T.pay[:, W * d:W * d + CAP], src, ActivationFunctionType.Copy).then_inc(sem, 1)
             k += 1
 
-    sent = 0
-    me = S["arr%d" % rank]
-    d0 = min(P["diag"])
-    g.wait_ge(S.ab, 8)
-    g.wait_ge(S.gd, 3)
-    rid, pid = topo.addr(P["relay"], core)
-    rm = topo.mask(core, P["relay"])
-    g.remote_dma(T.land[:, 0:3 * W], T.pay[:, W * d0:W * d0 + 3 * W], me, S.sent, pid, rid, rm)
+    g.wait_ge(S.ms, 3)
+    g.remote_dma(T.land[:, 0:36], T.msg[:, :], me, S.sent, r_pid, r_rid, rm)
     sent += _cnt(rm)
-    for ds, sem in groups[1:4]:
+    g.wait_ge(S.ab, 8)
+    for ds, sem in groups[0:3]:
         g.wait_ge(sem, len(ds))
         trs = []
         for d in ds:

@@ -3,12 +3,15 @@ from concourse.mybir import AluOpType, AxisListType, ActivationFunctionType
 
 N, RC, CAP = 12, 4096, 64
 W = CAP + 8
+BS = 2 * CAP + 8
+JUNK = RC + N * CAP
+WIN = JUNK + 16
 
 SCRATCH = {
-    "tabw": ("sbuf", [128, RC + CAP], "bfloat16"),
+    "tabw": ("sbuf", [128, WIN], "bfloat16"),
     "newb": ("sbuf", [128, 256], "bfloat16"),
-    "pay": ("sbuf", [128, N * W], "bfloat16"),
-    "land": ("sbuf", [128, N * W], "bfloat16"),
+    "pay": ("sbuf", [128, N * BS], "bfloat16"),
+    "land": ("sbuf", [128, 11 * W], "bfloat16"),
     "msg": ("sbuf", [128, 36], "bfloat16"),
     "col": ("sbuf", [128, 2], "int32"),
     "di": ("sbuf", [128, 2], "int32"),
@@ -36,7 +39,7 @@ SCRATCH = {
     "lh": ("sbuf", [128, 256], "bfloat16"),
     "rh": ("sbuf", [128, 288], "bfloat16"),
     "gl": ("sbuf", [128, 48], "uint16"),
-    "off": ("sbuf", [128, 48], "uint16"),
+    "off": ("sbuf", [128, 52], "uint16"),
     "ps1": ("psum", [128, 512], "float32"),
     "psg": ("psum", [128, 512], "float32"),
     "psab": ("psum", [128, 512], "float32"),
@@ -79,20 +82,32 @@ def _plan(s, cores, topo):
     oe = _engines(offm)
     pe = _engines(topo.mask(c, cores[peers[0]]) & ~offm)
     eng = {}
-    for k, d in enumerate(adj[0:4]):
-        eng[d] = _bits(oe[2 * k:2 * k + 2])
-    for k, d in enumerate(adj[4:6]):
-        eng[d] = _bits(oe[4 * k:4 * k + 4])
+    half = len(oe) // 2
+    for d in near:
+        eng[d] = _bits(oe[0:half])
+    for d in far:
+        eng[d] = _bits(oe[half:])
     for k, d in enumerate(peers):
         eng[d] = _bits(pe[4 * k:4 * k + 4])
     for d in diag:
         eng[d] = topo.mask(relay, cores[d])
-    return {"peers": peers, "adj": adj, "diag": diag, "relay": relay, "eng": eng}
+    return {"peers": peers, "adj": adj, "near": near, "far": far, "a": a, "diag": diag, "relay": relay, "eng": eng}
+
+
+def _layout(P):
+    a = P["a"]
+    groups = [[(P["peers"][0], "L", 0), (P["peers"][1], "R", W)]]
+    for r in range(3):
+        groups.append([(P["near"][(a - r) % 3], "L", 2 * W * (1 + r)), (P["far"][(a - r) % 3], "R", 2 * W * (1 + r) + W)])
+    groups.append([(s, "LRL"[k], 8 * W + W * k) for k, s in enumerate(P["diag"])])
+    return groups
 
 
 def rank_program(g, core, T, topo):
     cores = list(T.cores)
     plans = [_plan(s, cores, topo) for s in range(N)]
+    lays = [_layout(p) for p in plans]
+    spot = [dict((s, (f, c)) for grp in lay for s, f, c in grp) for lay in lays]
     rank = T.rank_of(core)
     S = T.sem
     A = AluOpType
@@ -105,7 +120,7 @@ def rank_program(g, core, T, topo):
             v, ac = g.vector, g.scalar
             cm = _cnt(topo.mask(cores[s], core))
             arr = S["arr%d" % s]
-            v.memset(T.bc[:, 0:4], 4096.0).then_inc(S.vs, 1)
+            v.memset(T.bc[:, 0:4], float(RC + CAP * s)).then_inc(S.vs, 1)
             g.iota(T.pidx[:, :], [[0, 4]], 0, 1).then_inc(S.c1, 1)
             g.iota(T.r16[:, :], [[16, 4]], 0, 0, allow_small_or_imprecise_dtypes=True).then_inc(S.c1, 1)
             v.wait_ge(S.c1, 2)
@@ -118,24 +133,32 @@ def rank_program(g, core, T, topo):
             v.wait_ge(arr, cm)
             v.tensor_copy(out=T.gl[:, 0:12], in_=T.land[:, 0:12]).then_inc(S.gls, 1)
             for k in range(3):
-                v.tensor_tensor(out=T.pay[:, W * k + CAP + 4:W * k + CAP + 8], in0=T.land[:, 24 + 4 * k:28 + 4 * k],
+                v.tensor_tensor(out=T.pay[:, BS * k + CAP + 4:BS * k + CAP + 8], in0=T.land[:, 24 + 4 * k:28 + 4 * k],
                                 in1=T.bc[:, 4:8], op=A.add).then_inc(S.ab, 1)
             ac.wait_ge(arr, cm)
             for k in range(3):
-                ac.activation(T.pay[:, W * k + CAP:W * k + CAP + 4], T.land[:, 12 + 4 * k:16 + 4 * k],
+                ac.activation(T.pay[:, BS * k + CAP:BS * k + CAP + 4], T.land[:, 12 + 4 * k:16 + 4 * k],
                               ActivationFunctionType.Identity, bias=T.bc[:, 0:1]).then_inc(S.ab, 1)
             v.wait_ge(S.gls, 1)
             v.wait_ge(S.raw, cm)
+            ac.wait_ge(S.gls, 1)
+            ac.wait_ge(S.raw, cm)
             done = (S.gd, S.g4, S.g2)
-            for k in range(3):
-                v.tensor_copy(out=T.pay[:, W * k:W * k + CAP],
-                              in_=T.newb[:, 0:256].indirect(T.gl[:, 4 * k:4 * k + 4])).then_inc(done[k], 1)
+            for k, d in enumerate(P["diag"]):
+                c = BS * k + (W if spot[d][s][0] == "L" else 0)
+                cols = T.newb[:, 0:256].indirect(T.gl[:, 4 * k:4 * k + 4])
+                if k == 1:
+                    ac.activation(T.pay[:, c:c + CAP], cols, ActivationFunctionType.Copy).then_inc(done[k], 1)
+                else:
+                    v.tensor_copy(out=T.pay[:, c:c + CAP], in_=cols).then_inc(done[k], 1)
             g.wait_ge(S.ab, 6)
             cnt = 0
             for k, d in enumerate(P["diag"]):
                 g.wait_ge(done[k], 1)
                 rid, pid = topo.addr(cores[d], core)
-                g.remote_dma(T.land[:, W * s:W * s + W], T.pay[:, W * k:W * k + W], arr, S.sent, pid, rid, P["eng"][d])
+                f, c = spot[d][s]
+                b = BS * k + (CAP if f == "L" else 0)
+                g.remote_dma(T.land[:, c:c + W], T.pay[:, b:b + W], arr, S.sent, pid, rid, P["eng"][d])
                 cnt += _cnt(P["eng"][d])
             g.wait_ge(S.sent, cnt)
         return
@@ -164,7 +187,7 @@ def rank_program(g, core, T, topo):
     g.sync.dma_start(T.tabw[:, 0:RC], T.tab[:, :]).then_inc(S.stab, 16)
 
     v.memset(T.ones[:, :], 1.0).then_inc(S.on, 1)
-    V(v.memset(T.bc[:, 0:4], 4096.0))
+    V(v.memset(T.bc[:, 0:4], float(RC + CAP * rank)))
     g.iota(T.pidx[:, :], [[0, 4]], 0, 1).then_inc(S.c1, 1)
     g.iota(T.jb[:, :], [[16, 2]], 0, 32, allow_small_or_imprecise_dtypes=True).then_inc(S.c1, 1)
     g.iota(T.r16[:, :], [[16, 4]], 0, 0, allow_small_or_imprecise_dtypes=True).then_inc(S.c1, 1)
@@ -194,6 +217,7 @@ def rank_program(g, core, T, topo):
     level()
     v_bc = n["v"]
     V(v.tensor_tensor(out=T.jf[:, :], in0=T.jf[:, :], in1=T.jb[:, :], op=A.add))
+    V(ts(T.off[:, 44:45], T.bc[:, 4:5], float(JUNK), A.add))
 
     v.wait_ge(S.spos, 16)
     V(ts(T.di[:, :], T.col[:, :], 12, A.logical_shift_right))
@@ -201,7 +225,7 @@ def rank_program(g, core, T, topo):
     V(ts(T.yi[:, 2:4], T.col[:, :], 63, A.bitwise_and))
     level()
     V(v.tensor_copy(out=T.df[:, :], in_=T.di[:, :]))
-    V(ts(T.af[:, :], T.yi[:, 0:2], -4032.0, A.add))
+    V(ts(T.af[:, :], T.yi[:, 0:2], float(CAP - RC - CAP * rank), A.add))
     V(v.tensor_copy(out=T.lof[:, :], in_=T.yi[:, 2:4]))
     level((S.c2, 3))
     V(ts(T.oh[:, 0:12], T.i12[:, :], T.df[:, 0:1], A.is_equal))
@@ -249,9 +273,10 @@ def rank_program(g, core, T, topo):
                       ActivationFunctionType.Copy).then_inc(S.ms, 1)
     ac.wait_ge(S.vs, v_bc)
     for k in range(8):
-        ac.activation(T.pay[:, CAP + k::W], T.psab[:, 48 * (k // 4) + k % 4:48 * (k // 4) + 48:4],
+        ac.activation(T.pay[:, CAP + k::BS], T.psab[:, 48 * (k // 4) + k % 4:48 * (k // 4) + 48:4],
                       ActivationFunctionType.Identity, bias=T.bc[:, k:k + 1]).then_inc(S.ab, 1)
-    groups = [(P["adj"][0:4], S.g4), (P["adj"][4:6], S.g2), (P["peers"], S.gp), ([rank], S.go)]
+    rounds = [[P["near"][(P["a"] + r) % 3], P["far"][(P["a"] + r) % 3]] for r in range(3)]
+    groups = [(rounds[0], S.gd), (rounds[1], S.g4), (rounds[2], S.g2), (P["peers"], S.gp), ([rank], S.go)]
     v.wait_ge(S.gls, 1)
     v.wait_ge(S.snew, 16)
     ac.wait_ge(S.gls, 1)
@@ -259,39 +284,49 @@ def rank_program(g, core, T, topo):
     k = 0
     for ds, sem in groups:
         for d in ds:
-            src = T.newb[:, 0:256].indirect(T.gl[:, 4 * d:4 * d + 4])
+            cols = T.newb[:, 0:256].indirect(T.gl[:, 4 * d:4 * d + 4])
+            c = BS * d + (W if d != rank and spot[d][rank][0] == "L" else 0)
             if k < 6:
-                v.tensor_copy(out=T.pay[:, W * d:W * d + CAP], in_=src).then_inc(sem, 1)
+                v.tensor_copy(out=T.pay[:, c:c + CAP], in_=cols).then_inc(sem, 1)
             else:
-                ac.activation(T.pay[:, W * d:W * d + CAP], src, ActivationFunctionType.Copy).then_inc(sem, 1)
+                ac.activation(T.pay[:, c:c + CAP], cols, ActivationFunctionType.Copy).then_inc(sem, 1)
             k += 1
 
     g.wait_ge(S.ms, 3)
     g.remote_dma(T.land[:, 0:36], T.msg[:, :], me, S.sent, r_pid, r_rid, rm)
     sent += _cnt(rm)
     g.wait_ge(S.ab, 8)
-    for ds, sem in groups[0:3]:
+    for ds, sem in (groups[0], groups[1], groups[3], groups[2]):
         g.wait_ge(sem, len(ds))
         trs = []
         for d in ds:
             rid, pid = topo.addr(cores[d], core)
+            f, c = spot[d][rank]
+            b = BS * d + (CAP if f == "L" else 0)
             trs.append(RemoteDMATransfer(dst_ids=[DstId(rid=rid, pnc=pid)], dma_engine_mask=P["eng"][d], remote_sem=me,
-                                         src=T.pay[:, W * d:W * d + W], dst=T.land[:, W * rank:W * rank + W]))
+                                         src=T.pay[:, b:b + W], dst=T.land[:, c:c + W]))
             sent += _cnt(P["eng"][d])
         g.remote_dma_fused(trs, local_sem=S.sent)
 
     v.wait_ge(S.stab, 16)
-    for s in [rank] + P["peers"] + P["adj"] + P["diag"]:
-        buf = T.pay if s == rank else T.land
-        if s == rank:
-            v.wait_ge(S.go, 1)
-            v.wait_ge(S.ab, 8)
-        else:
+    v.wait_ge(S.go, 1)
+    v.wait_ge(S.ab, 8)
+    b = BS * rank
+    V(v.tensor_tensor(out=T.off[:, 0:4], in0=T.pay[:, b + CAP:b + CAP + 4], in1=T.pay[:, b + CAP + 4:b + CAP + 8], op=A.add))
+    level()
+    V(v.tensor_copy(out=T.tabw[:, 0:WIN].indirect(T.off[:, 0:4]), in_=T.pay[:, b:b + CAP]))
+    c0 = 4
+    for grp in lays[rank]:
+        lo = grp[0][2] + 8
+        hi = grp[-1][2] + (W if grp[-1][1] == "L" else CAP)
+        for s, f, c in grp:
+            o = c if f == "L" else c + CAP
+            q = c0 + ((c + 8 if f == "L" else c) - lo) // 16
             v.wait_ge(S["arr%d" % s], _cnt(plans[s]["eng"][rank]))
-        V(v.tensor_tensor(out=T.off[:, 4 * s:4 * s + 4], in0=buf[:, W * s + CAP:W * s + CAP + 4],
-                          in1=buf[:, W * s + CAP + 4:W * s + CAP + 8], op=A.add))
+            V(v.tensor_tensor(out=T.off[:, q:q + 4], in0=T.land[:, o:o + 4], in1=T.land[:, o + 4:o + 8], op=A.add))
         level()
-        V(v.tensor_copy(out=T.tabw[:, 0:RC + CAP].indirect(T.off[:, 4 * s:4 * s + 4]), in_=buf[:, W * s:W * s + CAP]))
+        V(v.tensor_copy(out=T.tabw[:, 0:WIN].indirect(T.off[:, c0:c0 + (hi - lo) // 16]), in_=T.land[:, lo:hi]))
+        c0 += (hi - lo) // 16
 
     g.sync.wait_ge(S.vs, n["v"])
     g.sync.dma_start(T.y[:, :], T.tabw[:, 0:RC]).then_inc(S.sout, 16)

from concourse.bass import DstId, RemoteDMATransfer
from concourse.mybir import AluOpType, AxisListType, ActivationFunctionType

N, RC, CAP = 12, 4096, 64
W = CAP + 8
BS = 2 * CAP + 8
JUNK = RC + N * CAP
WIN = JUNK + 16

SCRATCH = {
    "tabw": ("sbuf", [128, WIN], "bfloat16"),
    "newb": ("sbuf", [128, 256], "bfloat16"),
    "pay": ("sbuf", [128, N * BS], "bfloat16"),
    "land": ("sbuf", [128, 11 * W], "bfloat16"),
    "msg": ("sbuf", [128, 36], "bfloat16"),
    "col": ("sbuf", [128, 2], "int32"),
    "di": ("sbuf", [128, 2], "int32"),
    "yi": ("sbuf", [128, 4], "int32"),
    "r16i": ("sbuf", [128, 2], "int32"),
    "pidx": ("sbuf", [128, 4], "int32"),
    "tmi": ("sbuf", [128, 8], "int32"),
    "df": ("sbuf", [128, 2], "float32"),
    "d4": ("sbuf", [128, 2], "float32"),
    "af": ("sbuf", [128, 2], "float32"),
    "lof": ("sbuf", [128, 2], "float32"),
    "bf": ("sbuf", [128, 2], "float32"),
    "jf": ("sbuf", [128, 2], "float32"),
    "jb": ("sbuf", [128, 2], "float32"),
    "rk": ("sbuf", [128, 2], "float32"),
    "abf": ("sbuf", [128, 4], "float32"),
    "bc": ("sbuf", [128, 8], "float32"),
    "r16": ("sbuf", [128, 4], "float32"),
    "i12": ("sbuf", [128, 12], "float32"),
    "i48": ("sbuf", [128, 48], "float32"),
    "tidx": ("sbuf", [128, 128], "bfloat16"),
    "ones": ("sbuf", [128, 128], "bfloat16"),
    "ltb": ("sbuf", [128, 128], "bfloat16"),
    "oh": ("sbuf", [128, 24], "bfloat16"),
    "lh": ("sbuf", [128, 256], "bfloat16"),
    "rh": ("sbuf", [128, 288], "bfloat16"),
    "gl": ("sbuf", [128, 48], "uint16"),
    "off": ("sbuf", [128, 52], "uint16"),
    "ps1": ("psum", [128, 512], "float32"),
    "psg": ("psum", [128, 512], "float32"),
    "psab": ("psum", [128, 512], "float32"),
}
SEMAPHORES = ["vs", "on", "c1", "c2", "c3", "p1", "h0", "h1", "p2", "gls", "ab", "gd", "g4", "g2", "gp", "go",
              "spos", "snew", "stab", "sout", "sent", "raw", "ms"] + ["arr%d" % s for s in range(N)]

RELAY_PICK = (0, 4, 2)


def _engines(mask):
    return [e for e in range(16) if (mask >> e) & 1]


def _bits(es):
    m = 0
    for e in es:
        m |= 1 << e
    return m


def _cnt(mask):
    return len(_engines(mask))


def _plan(s, cores, topo):
    c = cores[s]
    home = [d for d in range(N) if topo.host(cores[d]) == topo.host(c)]
    peers = [d for d in home if d != s]
    adj = [d for d in range(N) if d not in home and topo.may_write(c, cores[d])]
    diag = [d for d in range(N) if not topo.may_write(c, cores[d])]
    a = home.index(s)
    near = [d for d in adj if topo.rack(topo.host(cores[d])) == topo.rack(topo.host(c))]
    far = [d for d in adj if d not in near]
    via = (far if a == 1 else near)[0]
    idle = [x for x in range(max(cores) + 8) if topo.host(x) == topo.host(cores[via])
            and topo.chip(x) == topo.chip(cores[via]) and x not in cores]
    relay = idle[RELAY_PICK[a]]
    offm = topo.mask(c, cores[adj[0]])
    oe = _engines(offm)
    pe = _engines(topo.mask(c, cores[peers[0]]) & ~offm)
    eng = {}
    half = len(oe) // 2
    for d in near:
        eng[d] = _bits(oe[0:half])
    for d in far:
        eng[d] = _bits(oe[half:])
    for k, d in enumerate(peers):
        eng[d] = _bits(pe[4 * k:4 * k + 4])
    for d in diag:
        eng[d] = topo.mask(relay, cores[d])
    return {"peers": peers, "adj": adj, "near": near, "far": far, "a": a, "diag": diag, "relay": relay, "eng": eng}


def _layout(P):
    a = P["a"]
    groups = [[(P["peers"][0], "L", 0), (P["peers"][1], "R", W)]]
    for r in range(3):
        groups.append([(P["near"][(a - r) % 3], "L", 2 * W * (1 + r)), (P["far"][(a - r) % 3], "R", 2 * W * (1 + r) + W)])
    groups.append([(s, "LRL"[k], 8 * W + W * k) for k, s in enumerate(P["diag"])])
    return groups


def rank_program(g, core, T, topo):
    cores = list(T.cores)
    plans = [_plan(s, cores, topo) for s in range(N)]
    lays = [_layout(p) for p in plans]
    spot = [dict((s, (f, c)) for grp in lay for s, f, c in grp) for lay in lays]
    rank = T.rank_of(core)
    S = T.sem
    A = AluOpType

    if rank is None:
        for s in range(N):
            P = plans[s]
            if P["relay"] != core:
                continue
            v, ac = g.vector, g.scalar
            cm = _cnt(topo.mask(cores[s], core))
            arr = S["arr%d" % s]
            v.memset(T.bc[:, 0:4], float(RC + CAP * s)).then_inc(S.vs, 1)
            g.iota(T.pidx[:, :], [[0, 4]], 0, 1).then_inc(S.c1, 1)
            g.iota(T.r16[:, :], [[16, 4]], 0, 0, allow_small_or_imprecise_dtypes=True).then_inc(S.c1, 1)
            v.wait_ge(S.c1, 2)
            v.tensor_scalar(out=T.tmi[:, 0:4], in0=T.pidx[:, :], scalar1=15, scalar2=None,
                            op0=A.bitwise_and).then_inc(S.vs, 1)
            v.wait_ge(S.vs, 2)
            v.tensor_tensor(out=T.bc[:, 4:8], in0=T.tmi[:, 0:4], in1=T.r16[:, :], op=A.add).then_inc(S.vs, 1)
            v.wait_ge(S.vs, 3)
            ac.wait_ge(S.vs, 3)
            v.wait_ge(arr, cm)
            v.tensor_copy(out=T.gl[:, 0:12], in_=T.land[:, 0:12]).then_inc(S.gls, 1)
            for k in range(3):
                v.tensor_tensor(out=T.pay[:, BS * k + CAP + 4:BS * k + CAP + 8], in0=T.land[:, 24 + 4 * k:28 + 4 * k],
                                in1=T.bc[:, 4:8], op=A.add).then_inc(S.ab, 1)
            ac.wait_ge(arr, cm)
            for k in range(3):
                ac.activation(T.pay[:, BS * k + CAP:BS * k + CAP + 4], T.land[:, 12 + 4 * k:16 + 4 * k],
                              ActivationFunctionType.Identity, bias=T.bc[:, 0:1]).then_inc(S.ab, 1)
            v.wait_ge(S.gls, 1)
            v.wait_ge(S.raw, cm)
            ac.wait_ge(S.gls, 1)
            ac.wait_ge(S.raw, cm)
            done = (S.gd, S.g4, S.g2)
            for k, d in enumerate(P["diag"]):
                c = BS * k + (W if spot[d][s][0] == "L" else 0)
                cols = T.newb[:, 0:256].indirect(T.gl[:, 4 * k:4 * k + 4])
                if k == 1:
                    ac.activation(T.pay[:, c:c + CAP], cols, ActivationFunctionType.Copy).then_inc(done[k], 1)
                else:
                    v.tensor_copy(out=T.pay[:, c:c + CAP], in_=cols).then_inc(done[k], 1)
            g.wait_ge(S.ab, 6)
            cnt = 0
            for k, d in enumerate(P["diag"]):
                g.wait_ge(done[k], 1)
                rid, pid = topo.addr(cores[d], core)
                f, c = spot[d][s]
                b = BS * k + (CAP if f == "L" else 0)
                g.remote_dma(T.land[:, c:c + W], T.pay[:, b:b + W], arr, S.sent, pid, rid, P["eng"][d])
                cnt += _cnt(P["eng"][d])
            g.wait_ge(S.sent, cnt)
        return

    P = plans[rank]
    v, pe, ac = g.vector, g.tensor, g.scalar
    n = {"v": 0}

    def level(*deps):
        for sem, val in deps:
            v.wait_ge(sem, val)
        if n["v"]:
            v.wait_ge(S.vs, n["v"])

    def V(inst):
        inst.then_inc(S.vs, 1)
        n["v"] += 1

    def ts(out, in0, s1, op0, s2=None, op1=None):
        if op1 is None:
            return v.tensor_scalar(out=out, in0=in0, scalar1=s1, scalar2=None, op0=op0)
        return v.tensor_scalar(out=out, in0=in0, scalar1=s1, scalar2=s2, op0=op0, op1=op1)

    ac.dma_start(T.col[:, :], T.pos[:, :]).then_inc(S.spos, 16)
    g.sync.dma_start(T.newb[:, :], T.new[:, :]).then_inc(S.snew, 16)
    g.sync.dma_start(T.tabw[:, 0:RC], T.tab[:, :]).then_inc(S.stab, 16)

    v.memset(T.ones[:, :], 1.0).then_inc(S.on, 1)
    V(v.memset(T.bc[:, 0:4], float(RC + CAP * rank)))
    g.iota(T.pidx[:, :], [[0, 4]], 0, 1).then_inc(S.c1, 1)
    g.iota(T.jb[:, :], [[16, 2]], 0, 32, allow_small_or_imprecise_dtypes=True).then_inc(S.c1, 1)
    g.iota(T.r16[:, :], [[16, 4]], 0, 0, allow_small_or_imprecise_dtypes=True).then_inc(S.c1, 1)
    g.iota(T.i12[:, :], [[1, 12]], 0, 0, allow_small_or_imprecise_dtypes=True).then_inc(S.c2, 1)
    g.wait_ge(S.on, 1)
    g.affine_select(T.ltb[:, :], T.ones[:, :], [[1, 128]], A.is_gt, 0.0, 0, -1).then_inc(S.c2, 1)
    g.wait_ge(S.c2, 2)
    g.affine_select(T.ltb[:, :], T.ltb[:, :], [[1, 128]], A.not_equal, 64.0, 0, -1).then_inc(S.c2, 1)
    g.iota(T.i48[:, :], [[1, 48]], 0, 0, allow_small_or_imprecise_dtypes=True).then_inc(S.c3, 1)
    g.iota(T.tidx[:, :], [[0, 8], [1, 16]], 64, 0, allow_small_or_imprecise_dtypes=True).then_inc(S.c3, 1)

    sent = 0
    me = S["arr%d" % rank]
    d0 = min(P["diag"])
    r_rid, r_pid = topo.addr(P["relay"], core)
    rm = topo.mask(core, P["relay"])
    g.wait_ge(S.snew, 16)
    g.remote_dma(T.newb[:, :], T.newb[:, :], S.raw, S.sent, r_pid, r_rid, rm)
    sent += _cnt(rm)

    level((S.c1, 3))
    V(ts(T.tmi[:, 0:4], T.pidx[:, :], 15, A.bitwise_and))
    V(ts(T.tmi[:, 4:6], T.pidx[:, 0:2], 3, A.logical_shift_right))
    level()
    V(v.tensor_tensor(out=T.bc[:, 4:8], in0=T.tmi[:, 0:4], in1=T.r16[:, :], op=A.add))
    V(ts(T.jf[:, :], T.tmi[:, 4:6], -255.0, A.mult))
    level()
    v_bc = n["v"]
    V(v.tensor_tensor(out=T.jf[:, :], in0=T.jf[:, :], in1=T.jb[:, :], op=A.add))
    V(ts(T.off[:, 44:45], T.bc[:, 4:5], float(JUNK), A.add))

    v.wait_ge(S.spos, 16)
    V(ts(T.di[:, :], T.col[:, :], 12, A.logical_shift_right))
    V(ts(T.yi[:, 0:2], T.col[:, :], 4032, A.bitwise_and))
    V(ts(T.yi[:, 2:4], T.col[:, :], 63, A.bitwise_and))
    level()
    V(v.tensor_copy(out=T.df[:, :], in_=T.di[:, :]))
    V(ts(T.af[:, :], T.yi[:, 0:2], float(CAP - RC - CAP * rank), A.add))
    V(v.tensor_copy(out=T.lof[:, :], in_=T.yi[:, 2:4]))
    level((S.c2, 3))
    V(ts(T.oh[:, 0:12], T.i12[:, :], T.df[:, 0:1], A.is_equal))
    V(ts(T.oh[:, 12:24], T.i12[:, :], T.df[:, 1:2], A.is_equal))
    V(ts(T.d4[:, :], T.df[:, :], 4.0, A.mult))
    pe.wait_ge(S.c2, 3)
    pe.wait_ge(S.on, 1)
    pe.wait_ge(S.vs, n["v"])
    pe.matmul(T.ps1[:, 0:12], T.ltb[:, :], T.oh[:, 0:12], True, True).then_inc(S.p1, 1)
    pe.matmul(T.ps1[:, 12:24], T.ones[:, :], T.oh[:, 0:12], True, False)
    pe.matmul(T.ps1[:, 12:24], T.ltb[:, :], T.oh[:, 12:24], False, True).then_inc(S.p1, 1)
    v.wait_ge(S.p1, 2)
    V(v.tensor_reduce(out=T.rk[:, 0:1], in_=T.ps1[:, 0:12], axis=AxisListType.X, op=A.max))
    V(v.tensor_reduce(out=T.rk[:, 1:2], in_=T.ps1[:, 12:24], axis=AxisListType.X, op=A.max))
    level()
    V(ts(T.r16i[:, :], T.rk[:, :], 0.0625, A.mult, -4.46875, A.add))
    V(v.tensor_tensor(out=T.bf[:, :], in0=T.lof[:, :], in1=T.rk[:, :], op=A.subtract))
    level()
    V(v.tensor_tensor(out=T.abf[:, 0:2], in0=T.r16i[:, :], in1=T.d4[:, :], op=A.add))
    for h in range(2):
        V(ts(T.abf[:, 2 + h:3 + h], T.r16i[:, h:h + 1], -16.0, A.mult, T.rk[:, h:h + 1], A.add))

    level((S.c3, 2))
    vals = (T.jf, T.af, T.bf)
    for h in range(2):
        hs = S["h%d" % h]
        ts(T.lh[:, 128 * h:128 * h + 128], T.tidx[:, :], T.abf[:, 2 + h:3 + h], A.is_equal).then_inc(hs, 1)
        for q in range(3):
            ts(T.rh[:, 144 * h + 48 * q:144 * h + 48 * q + 48], T.i48[:, :], T.abf[:, h:h + 1], A.is_equal,
               vals[q][:, h:h + 1], A.mult).then_inc(hs, 1)
        pe.wait_ge(hs, 4)
        m1 = pe.matmul(T.psg[:, 0:48], T.lh[:, 128 * h:128 * h + 128], T.rh[:, 144 * h:144 * h + 48], h == 0, h == 1)
        m2 = pe.matmul(T.psab[:, 0:96], T.lh[:, 128 * h:128 * h + 128], T.rh[:, 144 * h + 48:144 * h + 144],
                       h == 0, h == 1)
        if h == 1:
            m1.then_inc(S.p2, 1)
            m2.then_inc(S.p2, 1)

    v.wait_ge(S.p2, 2)
    v.tensor_copy(out=T.msg[:, 0:12], in_=T.psg[:, 4 * d0:4 * d0 + 12]).then_inc(S.ms, 1)
    v.tensor_copy(out=T.gl[:, :], in_=T.psg[:, 0:48]).then_inc(S.gls, 1)
    ac.wait_ge(S.p2, 2)
    for q in range(2):
        ac.activation(T.msg[:, 12 + 12 * q:24 + 12 * q], T.psab[:, 48 * q + 4 * d0:48 * q + 4 * d0 + 12],
                      ActivationFunctionType.Copy).then_inc(S.ms, 1)
    ac.wait_ge(S.vs, v_bc)
    for k in range(8):
        ac.activation(T.pay[:, CAP + k::BS], T.psab[:, 48 * (k // 4) + k % 4:48 * (k // 4) + 48:4],
                      ActivationFunctionType.Identity, bias=T.bc[:, k:k + 1]).then_inc(S.ab, 1)
    rounds = [[P["near"][(P["a"] + r) % 3], P["far"][(P["a"] + r) % 3]] for r in range(3)]
    groups = [(rounds[0], S.gd), (rounds[1], S.g4), (rounds[2], S.g2), (P["peers"], S.gp), ([rank], S.go)]
    v.wait_ge(S.gls, 1)
    v.wait_ge(S.snew, 16)
    ac.wait_ge(S.gls, 1)
    ac.wait_ge(S.snew, 16)
    k = 0
    for ds, sem in groups:
        for d in ds:
            cols = T.newb[:, 0:256].indirect(T.gl[:, 4 * d:4 * d + 4])
            c = BS * d + (W if d != rank and spot[d][rank][0] == "L" else 0)
            if k < 6:
                v.tensor_copy(out=T.pay[:, c:c + CAP], in_=cols).then_inc(sem, 1)
            else:
                ac.activation(T.pay[:, c:c + CAP], cols, ActivationFunctionType.Copy).then_inc(sem, 1)
            k += 1

    g.wait_ge(S.ms, 3)
    g.remote_dma(T.land[:, 0:36], T.msg[:, :], me, S.sent, r_pid, r_rid, rm)
    sent += _cnt(rm)
    g.wait_ge(S.ab, 8)
    for ds, sem in (groups[0], groups[1], groups[3], groups[2]):
        g.wait_ge(sem, len(ds))
        trs = []
        for d in ds:
            rid, pid = topo.addr(cores[d], core)
            f, c = spot[d][rank]
            b = BS * d + (CAP if f == "L" else 0)
            trs.append(RemoteDMATransfer(dst_ids=[DstId(rid=rid, pnc=pid)], dma_engine_mask=P["eng"][d], remote_sem=me,
                                         src=T.pay[:, b:b + W], dst=T.land[:, c:c + W]))
            sent += _cnt(P["eng"][d])
        g.remote_dma_fused(trs, local_sem=S.sent)

    v.wait_ge(S.stab, 16)
    v.wait_ge(S.go, 1)
    v.wait_ge(S.ab, 8)
    b = BS * rank
    V(v.tensor_tensor(out=T.off[:, 0:4], in0=T.pay[:, b + CAP:b + CAP + 4], in1=T.pay[:, b + CAP + 4:b + CAP + 8], op=A.add))
    level()
    V(v.tensor_copy(out=T.tabw[:, 0:WIN].indirect(T.off[:, 0:4]), in_=T.pay[:, b:b + CAP]))
    c0 = 4
    for grp in lays[rank]:
        lo = grp[0][2] + 8
        hi = grp[-1][2] + (W if grp[-1][1] == "L" else CAP)
        for s, f, c in grp:
            o = c if f == "L" else c + CAP
            q = c0 + ((c + 8 if f == "L" else c) - lo) // 16
            v.wait_ge(S["arr%d" % s], _cnt(plans[s]["eng"][rank]))
            V(v.tensor_tensor(out=T.off[:, q:q + 4], in0=T.land[:, o:o + 4], in1=T.land[:, o + 4:o + 8], op=A.add))
        level()
        V(v.tensor_copy(out=T.tabw[:, 0:WIN].indirect(T.off[:, c0:c0 + (hi - lo) // 16]), in_=T.land[:, lo:hi]))
        c0 += (hi - lo) // 16

    g.sync.wait_ge(S.vs, n["v"])
    g.sync.dma_start(T.y[:, :], T.tabw[:, 0:RC]).then_inc(S.sout, 16)
    g.sync.wait_ge(S.sout, 16)
    g.wait_ge(S.sent, sent)
